import numpy as np
import ml_dtypes


def mxq(x, axis, fmt="e4m3"):
    dtype, down = {"e4m3": (ml_dtypes.float8_e4m3fn, 7), "e5m2": (ml_dtypes.float8_e5m2, 14)}[fmt]
    v = np.moveaxis(np.asarray(x, np.float32).astype(ml_dtypes.bfloat16).astype(np.float64), axis, -1)
    blocks = v.reshape(v.shape[:-1] + (-1, 32))
    amax = np.abs(blocks).max(-1, keepdims=True)
    byte = np.maximum(np.where(amax > 0, np.frexp(amax)[1] - 1 + 127, 0) - down, 1)
    scale = np.exp2(byte - 127.0)
    codes = (blocks / scale).astype(np.float32).astype(dtype).astype(np.float64)
    return np.moveaxis((codes * scale).reshape(v.shape), -1, axis)


WIDE = False


def mx_kscale(k):
    if not WIDE:
        return np.ones(k)
    levels = np.array([10, -10, 5, -5, 0])
    if k % 512:
        return np.exp2(np.random.permutation(np.resize(levels, k // 32))).repeat(32)
    a = np.empty((k // 512, 16))
    for p in range(k // 512):
        a[p, :8] = np.random.permutation(np.resize(levels, 8))
        for g in range(8):
            far = levels[np.abs(levels - a[p, g]) >= 10]
            a[p, g + 8] = far[np.random.randint(len(far))]
    return np.exp2(a.ravel()).repeat(32)


def f64(x):
    return np.asarray(x).astype(np.float64)


def striped(idx):
    return np.tile(idx.reshape(-1, 16).T, (8, 1)).astype(np.uint16)


def unstriped(offs):
    return offs[:16].T.reshape(-1).astype(np.int64)


def striped8(idx):
    return np.concatenate([x.reshape(-1, 16).T for x in idx]).astype(np.uint16)


def runs(offs, k):
    lists = np.stack([offs[16 * r : 16 * r + 16].T.reshape(-1) for r in range(8)]).astype(np.int64)
    return lists[np.arange(k) % 512 // 64]


def pack_weight(w):
    k, n = w.shape
    w = f64(np.asarray(w, np.float32).astype(ml_dtypes.bfloat16)).reshape(k // 32, 32, n)
    amax = np.abs(w).max(1)
    byte = np.clip(np.where(amax > 0, np.frexp(amax)[1] - 1 + 127 - 7, 1), 1, 254)
    scaled = (w * np.exp2(127.0 - byte)[:, None, :]).reshape(k, n).astype(np.float32)
    words = np.ascontiguousarray(scaled.reshape(k // 512, 128, 4, n).transpose(0, 1, 3, 2)).astype(ml_dtypes.float8_e4m3fn).view(np.uint8)
    return words, np.ascontiguousarray(byte.astype(np.uint8).reshape(k // 512, 16, n))


def unpack_weight(words, scales):
    g, p, n, _ = words.shape
    vals = np.ascontiguousarray(words).view(ml_dtypes.float8_e4m3fn).astype(np.float64) * np.repeat(np.exp2(scales.astype(np.float64) - 127.0), 8, axis=1)[..., None]
    return vals.transpose(0, 1, 3, 2).reshape(g * 512, n)


K, T, S, H, G = 512, 1024, 256, 512, 2048


def setup_inputs():
    n = np.random.standard_normal
    s = mx_kscale(K)[:, None]
    packed_xT = pack_weight(n((K, T)) * s)
    packed_dT = pack_weight(n((K, G)) / s)
    return {
        "x_words": packed_xT[0],
        "x_scales": packed_xT[1],
        "w1": (n((K, H)) / np.sqrt(K) / s).astype(np.float32),
        "w2": (n((K, H)) / np.sqrt(K) / s).astype(np.float32),
        "gs": (np.random.uniform(0.5, 1.5, (K, 1)) * s).astype(np.float32),
        "d_words": packed_dT[0],
        "d_scales": packed_dT[1],
        "offs": striped(np.random.permutation(T)[:S]),
        "two": striped(np.random.permutation(T)[:S]),
        "n1": striped8(np.stack([np.random.permutation(S) for _ in range(8)])),
        "n2": striped8(np.stack([np.random.permutation(S) for _ in range(8)])),
        "n3": striped8(np.stack([np.random.permutation(S) for _ in range(8)])),
        "k1": striped8(np.random.randint(0, G, (8, H))),
        "n4": striped(np.random.permutation(S)),
        "n5": striped(np.random.permutation(S)),
    }


def reference(x_words, x_scales, w1, w2, gs, d_words, d_scales, offs, two, n1, n2, n3, k1, n4, n5):
    d_k1 = unpack_weight(d_words, d_scales)[np.arange(K)[:, None], runs(k1, K)]
    x_two = unpack_weight(x_words, x_scales)[:, unstriped(two)]
    d = mxq(f64(w2), 0, "e4m3").T @ x_two
    xq = unpack_weight(x_words, x_scales)[:, unstriped(offs)]
    y = mxq(f64(w1), 0, "e4m3").T @ xq
    z = f64(gs) * (d * (y[np.arange(H)[:, None], runs(n1, H)] - y) + 0.5 * ((d[np.arange(H)[:, None], runs(n3, H)]) * (y[np.arange(H)[:, None], runs(n2, H)] - y)))
    h = 0.0625 * ((d_k1.T @ mxq(z, 0, "e4m3")))
    ex = np.exp(0.5 * h)
    return (2.0 * ex) / (ex + ex[:, unstriped(n4)] + ex[:, unstriped(n5)])

@@ -1,0 +1,221 @@
+from contextlib import ExitStack
+
+import concourse.mybir as mybir
+
+K, T, S, H, G = 512, 1024, 256, 512, 2048
+FLOPS = 3 * 2 * K * H * S
+
+F32 = mybir.dt.float32
+BF16 = mybir.dt.bfloat16
+I32 = mybir.dt.int32
+U32 = mybir.dt.uint32
+U16 = mybir.dt.uint16
+U8 = mybir.dt.uint8
+FP8X4 = mybir.dt.float8_e4m3fn_x4
+ACT = mybir.ActivationFunctionType
+ALU = mybir.AluOpType
+
+P = 128
+PACK = 4
+WINDOW = 2 * S
+HALF = S // 2
+
+
+def tile_picked_twqflowbshare_none_p_kernel(
+    tc, x_words, x_scales, w1, w2, gs, d_words, d_scales, offs, two, n1, n2, n3, k1, n4, n5, out
+):
+    nc = tc.nc
+    with ExitStack() as ctx:
+        keep = ctx.enter_context(tc.tile_pool(name="keep", bufs=1))
+        psum = ctx.enter_context(tc.psum_pool(name="psum", bufs=1))
+
+        def sb(name, shape, dtype):
+            return keep.tile(shape, dtype, name=name, align_bytes=64)
+
+        def load_list(name, src):
+            tile = keep.tile([P, src.shape[1]], U16, name=name)
+            nc.sync.dma_start(tile[:], src)
+            return tile
+
+        def load_weight_half(name, w, c):
+            raw = sb(name, [P, PACK, H // 2], F32)
+            cols = slice(c * H // 2, (c + 1) * H // 2)
+            nc.sync.dma_start(raw[:], w.rearrange("(p j) c -> p j c", j=PACK)[:, :, cols])
+            return raw
+
+        x_bytes = sb("x_bytes", [P, T], U8)
+        d_bytes = sb("d_bytes", [P, G], U8)
+        dk_scales = sb("dk_scales", [P, H], U8)
+        y_win = [sb("y_win%d" % t, [P, WINDOW], F32) for t in range(PACK)]
+        d_win = [sb("d_win%d" % t, [P, WINDOW], F32) for t in range(PACK)]
+        e_win = [sb("e_win%d" % m, [P, WINDOW], F32) for m in range(PACK)]
+        nc.vector.memset(x_bytes[:].bitcast(I32), 0)
+        nc.vector.memset(d_bytes[:].bitcast(I32), 0)
+        for win in y_win + d_win:
+            nc.vector.memset(win[:, S:], 0.0)
+        half = sb("half", [P, 1], F32)
+        nc.gpsimd.memset(half[:], 0.5)
+        nc.gpsimd.memset(dk_scales[:].bitcast(I32), 0)
+        for win in e_win:
+            nc.gpsimd.memset(win[:, S:], 0.0)
+
+        offs_sb = load_list("offs_sb", offs)
+        for q in range(4):
+            nc.scalar.dma_start(
+                x_bytes[32 * q : 32 * q + 4, :].bitcast(I32), x_scales[0, 4 * q : 4 * q + 4, :].bitcast(I32)
+            )
+        x_table = sb("x_table", [P, T], I32)
+        nc.sync.dma_start(x_table[:], x_words[0].rearrange("p n t -> p (n t)").bitcast(I32))
+        two_sb = load_list("two_sb", two)
+        w1_raw = [load_weight_half("w1_raw%d" % c, w1, c) for c in range(2)]
+        n2_sb = load_list("n2_sb", n2)
+        n1_sb = load_list("n1_sb", n1)
+        w2_raw = [load_weight_half("w2_raw%d" % c, w2, c) for c in range(2)]
+        gs_sb = sb("gs_sb", [P, PACK], F32)
+        nc.sync.dma_start(gs_sb[:], gs.rearrange("(p t) o -> p (t o)", t=PACK))
+        k1_sb = load_list("k1_sb", k1)
+        nc.sync.dma_start(d_bytes[0:P:8, :].bitcast(I32), d_scales[0].bitcast(I32))
+        n3_sb = load_list("n3_sb", n3)
+        d_table = sb("d_table", [P, G], I32)
+        nc.sync.dma_start(d_table[:], d_words[0].rearrange("p n t -> p (n t)").bitcast(I32))
+        n4_sb = load_list("n4_sb", n4)
+        n5_sb = load_list("n5_sb", n5)
+
+        def gather_bytes(name, table, offsets, n):
+            picked = sb(name, [P, n], U8)
+            nc.vector.tensor_copy(picked[:], table[:].indirect(offsets[:]))
+            return picked
+
+        def gather_words(name, table, offsets, n):
+            picked = sb(name, [P, n], U32)
+            nc.vector.tensor_copy(picked[:], table[:].bitcast(U32).indirect(offsets[:]))
+            return picked
+
+        def round_weight(name, raw, split):
+            grouped = sb(name, [P, PACK, P, PACK], BF16)
+            for c in range(2):
+                src = raw[c][:].rearrange("p j (m t) -> p m j t", t=PACK)
+                dst = grouped[:, :, c * 64 : (c + 1) * 64, :].rearrange("p t m j -> p m j t")
+                nc.vector.tensor_copy(dst[:, :split], src[:, :split])
+                if split < 64:
+                    nc.scalar.activation(dst[:, split:], src[:, split:], ACT.Copy)
+            return grouped
+
+        def project(name, grouped, words, scales):
+            codes = sb(name + "_codes", [P, PACK, P], U32)
+            planes = sb(name + "_planes", [P, PACK, P], U8)
+            banks = [psum.tile([P, 2, S], F32, name=name + "_bank%d" % b) for b in range(2)]
+            for b in range(2):
+                pair = slice(2 * b, 2 * b + 2)
+                nc.vector.quantize_mx(
+                    out=codes[:, pair, :].rearrange("p t m -> p (t m)").bitcast(FP8X4),
+                    scales=planes[:, pair, :].rearrange("p t m -> p (t m)"),
+                    in_=grouped[:, pair].rearrange("p t m j -> p (t m j)"),
+                )
+            for t in range(PACK):
+                nc.tensor.matmul_mx(
+                    out=banks[t // 2][:, t % 2, :],
+                    lhsT=codes[:, t, :].bitcast(FP8X4),
+                    lhsT_scale=planes[:, t, :],
+                    rhs=words[:].bitcast(FP8X4),
+                    rhs_scale=scales[:],
+                    start=True,
+                    stop=True,
+                )
+            return banks
+
+        xq_scales = gather_bytes("xq_scales", x_bytes, offs_sb, S)
+        xq_words = gather_words("xq_words", x_table, offs_sb, S)
+        x2_scales = gather_bytes("x2_scales", x_bytes, two_sb, S)
+        x2_words = gather_words("x2_words", x_table, two_sb, S)
+
+        y_banks = project("y", round_weight("w1_bf", w1_raw, 44), xq_words, xq_scales)
+        for t in range(PACK):
+            nc.scalar.activation(y_win[t][:, :S], y_banks[t // 2][:, t % 2, :], ACT.Copy)
+
+        y_n1 = sb("y_n1", [P, PACK, S], F32)
+        y_n2 = sb("y_n2", [P, PACK, S], F32)
+        for t in range(PACK):
+            nc.scalar.activation(y_n2[:, t, :], y_win[t][:].indirect(n2_sb[:]), ACT.Copy)
+            nc.scalar.activation(y_n1[:, t, :], y_win[t][:].indirect(n1_sb[:]), ACT.Copy)
+
+        d_banks = project("d", round_weight("w2_bf", w2_raw, 64), x2_words, x2_scales)
+        for t in range(PACK):
+            nc.scalar.activation(d_win[t][:, :S], d_banks[t // 2][:, t % 2, :], ACT.Copy, scale=gs_sb[:, t : t + 1])
+
+        dk_picked = gather_bytes("dk_picked", d_bytes, k1_sb, H)
+        for i in range(4):
+            nc.sync.dma_start(dk_scales[i:P:32, :].bitcast(I32), dk_picked[8 * i : P : 32, :].bitcast(I32))
+
+        diff1 = sb("diff1", [P, PACK, S], F32)
+        diff2 = sb("diff2", [P, PACK, S], F32)
+        for b in range(2):
+            pair = slice(2 * b, 2 * b + 2)
+            nc.vector.tensor_tensor(diff2[:, pair, :], y_n2[:, pair, :], y_banks[b][:], ALU.subtract)
+            nc.vector.tensor_tensor(diff1[:, pair, :], y_n1[:, pair, :], y_banks[b][:], ALU.subtract)
+
+        dk_words = gather_words("dk_words", d_table, k1_sb, H)
+
+        term1 = sb("term1", [P, PACK, S], F32)
+        for t in range(PACK):
+            nc.vector.tensor_tensor(term1[:, t, :], diff1[:, t, :], d_win[t][:, :S], ALU.mult)
+
+        e_inv = sb("e_inv", [P, PACK, S], F32)
+        for h in range(2):
+            cols = slice(h * HALF, (h + 1) * HALF)
+            d_n3 = sb("d_n3_%d" % h, [P, PACK, HALF], F32)
+            for t in range(PACK):
+                nc.scalar.activation(
+                    d_n3[:, t, :], d_win[t][:].indirect(n3_sb[:, h * HALF // 16 : (h + 1) * HALF // 16]), ACT.Copy
+                )
+            term2 = sb("term2_%d" % h, [P, PACK, HALF], F32)
+            for b in range(2):
+                pair = slice(2 * b, 2 * b + 2)
+                nc.vector.scalar_tensor_tensor(
+                    term2[:, pair, :], d_n3[:, pair, :], 0.5, diff2[:, pair, cols], ALU.mult, ALU.mult
+                )
+            z_bf = sb("z_bf%d" % h, [P, HALF, PACK], BF16)
+            nc.vector.tensor_tensor(
+                z_bf[:].rearrange("p (c i) t -> p c t i", i=4),
+                term1[:, :, cols].rearrange("p t (c i) -> p c t i", i=4),
+                term2[:].rearrange("p t (c i) -> p c t i", i=4),
+                ALU.add,
+            )
+            z_codes = sb("z_codes%d" % h, [P, HALF], U32)
+            z_plane = sb("z_plane%d" % h, [P, HALF], U8)
+            nc.vector.quantize_mx(
+                out=z_codes[:].bitcast(FP8X4), scales=z_plane[:], in_=z_bf[:].rearrange("p j t -> p (j t)")
+            )
+            banks = [psum.tile([P, 2, HALF], F32, name="h_bank%d_%d" % (h, b)) for b in range(2)]
+            for m in range(PACK):
+                rows = slice(m * P, (m + 1) * P)
+                nc.tensor.matmul_mx(
+                    out=banks[m // 2][:, m % 2, :],
+                    lhsT=dk_words[:, rows].bitcast(FP8X4),
+                    lhsT_scale=dk_scales[:, rows],
+                    rhs=z_codes[:].bitcast(FP8X4),
+                    rhs_scale=z_plane[:],
+                    start=True,
+                    stop=True,
+                )
+            for m in range(PACK):
+                nc.scalar.activation(e_win[m][:, cols], banks[m // 2][:, m % 2, :], ACT.Exp, scale=0.5 * 0.0625)
+            for b in range(2):
+                nc.scalar.activation(e_inv[:, 2 * b : 2 * b + 2, cols], banks[b][:], ACT.Exp, scale=-0.5 * 0.0625)
+
+        e_n4 = sb("e_n4", [P, PACK, S], F32)
+        for m in range(PACK):
+            nc.scalar.activation(e_n4[:, m, :], e_win[m][:].indirect(n4_sb[:]), ACT.Copy)
+        e_n45 = sb("e_n45", [P, PACK, S], F32)
+        ratio = sb("ratio", [P, PACK, S], F32)
+        for m in range(PACK + 1):
+            if m < PACK:
+                nc.vector.tensor_tensor(e_n45[:, m, :], e_win[m][:].indirect(n5_sb[:]), e_n4[:, m, :], ALU.add)
+            if m > 0:
+                nc.vector.tensor_tensor(ratio[:, m - 1, :], e_n45[:, m - 1, :], e_inv[:, m - 1, :], ALU.mult)
+        root = sb("root", [P, PACK, S], F32)
+        res = sb("res", [P, PACK, S], F32)
+        for m in range(PACK):
+            nc.scalar.activation(root[:, m, :], ratio[:, m, :], ACT.Abs_reciprocal_sqrt, scale=0.5, bias=half[:])
+            nc.vector.tensor_tensor(res[:, m, :], root[:, m, :], root[:, m, :], ALU.mult)
+            nc.sync.dma_start(out[m * P : (m + 1) * P, :], res[:, m, :])

@@ -29,137 +29,139 @@ def tile_picked_twqflowbshare_none_p_kernel(
         keep = ctx.enter_context(tc.tile_pool(name="keep", bufs=1))
         psum = ctx.enter_context(tc.psum_pool(name="psum", bufs=1))
 
-        def sb(name, shape, dtype):
-            return keep.tile(shape, dtype, name=name, align_bytes=64)
+        def sb(name, shape, dtype, tag=None):
+            return keep.tile(shape, dtype, name=name, tag=tag or name, align_bytes=64)
 
         def load_list(name, src):
             tile = keep.tile([P, src.shape[1]], U16, name=name)
             nc.sync.dma_start(tile[:], src)
             return tile
 
-        def load_weight_half(name, w, c):
-            raw = sb(name, [P, PACK, H // 2], F32)
-            cols = slice(c * H // 2, (c + 1) * H // 2)
-            nc.sync.dma_start(raw[:], w.rearrange("(p j) c -> p j c", j=PACK)[:, :, cols])
-            return raw
+        def load_weight_part(name, w, m0, m1):
+            raw = sb(name, [P, PACK, PACK * (m1 - m0)], F32)
+            nc.sync.dma_start(raw[:], w.rearrange("(p j) c -> p j c", j=PACK)[:, :, PACK * m0 : PACK * m1])
+            return raw, m0, m1
 
         x_bytes = sb("x_bytes", [P, T], U8)
         d_bytes = sb("d_bytes", [P, G], U8)
         dk_scales = sb("dk_scales", [P, H], U8)
         y_win = [sb("y_win%d" % t, [P, WINDOW], F32) for t in range(PACK)]
         d_win = [sb("d_win%d" % t, [P, WINDOW], F32) for t in range(PACK)]
-        e_win = [sb("e_win%d" % m, [P, WINDOW], F32) for m in range(PACK)]
-        nc.vector.memset(x_bytes[:].bitcast(I32), 0)
-        nc.vector.memset(d_bytes[:].bitcast(I32), 0)
-        for win in y_win + d_win:
-            nc.vector.memset(win[:, S:], 0.0)
+        e_win = [sb("e_win%d" % m, [P, S + 16], F32) for m in range(PACK)]
         half = sb("half", [P, 1], F32)
-        nc.gpsimd.memset(half[:], 0.5)
+        gs_sb = sb("gs_sb", [P, PACK], F32)
+        nc.gpsimd.memset(x_bytes[:].bitcast(I32), 0)
+        nc.vector.memset(d_bytes[:].bitcast(I32), 0)
+        for win in y_win + e_win:
+            nc.vector.memset(win[:, S:], 0.0)
+        nc.vector.memset(half[:], 0.5)
         nc.gpsimd.memset(dk_scales[:].bitcast(I32), 0)
-        for win in e_win:
+        for win in d_win:
             nc.gpsimd.memset(win[:, S:], 0.0)
+        nc.gpsimd.dma_start(gs_sb[:], gs.rearrange("(p t) o -> p (t o)", t=PACK))
+        nc.gpsimd.dma_start(d_bytes[0:P:8, :].bitcast(I32), d_scales[0].bitcast(I32))
 
         offs_sb = load_list("offs_sb", offs)
-        for q in range(4):
-            nc.scalar.dma_start(
-                x_bytes[32 * q : 32 * q + 4, :].bitcast(I32), x_scales[0, 4 * q : 4 * q + 4, :].bitcast(I32)
-            )
+        two_sb = load_list("two_sb", two)
         x_table = sb("x_table", [P, T], I32)
         nc.sync.dma_start(x_table[:], x_words[0].rearrange("p n t -> p (n t)").bitcast(I32))
-        two_sb = load_list("two_sb", two)
-        w1_raw = [load_weight_half("w1_raw%d" % c, w1, c) for c in range(2)]
-        n2_sb = load_list("n2_sb", n2)
-        n1_sb = load_list("n1_sb", n1)
-        w2_raw = [load_weight_half("w2_raw%d" % c, w2, c) for c in range(2)]
-        gs_sb = sb("gs_sb", [P, PACK], F32)
-        nc.sync.dma_start(gs_sb[:], gs.rearrange("(p t) o -> p (t o)", t=PACK))
+        for q in range(4):
+            nc.sync.dma_start(
+                x_bytes[32 * q : 32 * q + 4, :].bitcast(I32), x_scales[0, 4 * q : 4 * q + 4, :].bitcast(I32)
+            )
+        w1_raw = [load_weight_part("w1_raw%d" % m0, w1, m0, m0 + 64) for m0 in (0, 64)]
+        w2_raw = [load_weight_part("w2_raw0", w2, 0, 32), load_weight_part("w2_raw32", w2, 32, 80)]
         k1_sb = load_list("k1_sb", k1)
-        nc.sync.dma_start(d_bytes[0:P:8, :].bitcast(I32), d_scales[0].bitcast(I32))
-        n3_sb = load_list("n3_sb", n3)
+        n1_sb = load_list("n1_sb", n1)
+        n2_sb = load_list("n2_sb", n2)
+        w2_raw.append(load_weight_part("w2_raw80", w2, 80, 128))
         d_table = sb("d_table", [P, G], I32)
         nc.sync.dma_start(d_table[:], d_words[0].rearrange("p n t -> p (n t)").bitcast(I32))
+        n3_sb = load_list("n3_sb", n3)
         n4_sb = load_list("n4_sb", n4)
         n5_sb = load_list("n5_sb", n5)
 
-        def gather_bytes(name, table, offsets, n):
-            picked = sb(name, [P, n], U8)
+        def gather_bytes(name, table, offsets, n, tag=None):
+            picked = sb(name, [P, n], U8, tag=tag)
             nc.vector.tensor_copy(picked[:], table[:].indirect(offsets[:]))
             return picked
 
-        def gather_words(name, table, offsets, n):
-            picked = sb(name, [P, n], U32)
+        def gather_words(name, table, offsets, n, tag=None):
+            picked = sb(name, [P, n], U32, tag=tag)
             nc.vector.tensor_copy(picked[:], table[:].bitcast(U32).indirect(offsets[:]))
             return picked
 
-        def round_weight(name, raw, split):
-            grouped = sb(name, [P, PACK, P, PACK], BF16)
-            for c in range(2):
-                src = raw[c][:].rearrange("p j (m t) -> p m j t", t=PACK)
-                dst = grouped[:, :, c * 64 : (c + 1) * 64, :].rearrange("p t m j -> p m j t")
-                nc.vector.tensor_copy(dst[:, :split], src[:, :split])
-                if split < 64:
-                    nc.scalar.activation(dst[:, split:], src[:, split:], ACT.Copy)
-            return grouped
+        def round_part(on_vector, grouped, part, t0, t1):
+            raw, m0, m1 = part
+            src = raw[:].rearrange("p j (m t) -> p m j t", t=PACK)[:, :, :, t0:t1]
+            dst = grouped[:, :, m0:m1, :].rearrange("p t m j -> p m j t")
+            if on_vector:
+                nc.vector.tensor_copy(dst, src)
+            else:
+                nc.scalar.activation(dst, src, ACT.Copy)
 
-        def project(name, grouped, words, scales):
-            codes = sb(name + "_codes", [P, PACK, P], U32)
-            planes = sb(name + "_planes", [P, PACK, P], U8)
-            banks = [psum.tile([P, 2, S], F32, name=name + "_bank%d" % b) for b in range(2)]
+        def project(name, pairs, words, scales):
+            banks = []
             for b in range(2):
-                pair = slice(2 * b, 2 * b + 2)
+                codes = sb(name + "_codes%d" % b, [P, 2 * P], U32)
+                plane = sb(name + "_plane%d" % b, [P, 2 * P], U8)
                 nc.vector.quantize_mx(
-                    out=codes[:, pair, :].rearrange("p t m -> p (t m)").bitcast(FP8X4),
-                    scales=planes[:, pair, :].rearrange("p t m -> p (t m)"),
-                    in_=grouped[:, pair].rearrange("p t m j -> p (t m j)"),
+                    out=codes[:].bitcast(FP8X4), scales=plane[:], in_=pairs[b].rearrange("p t m j -> p (t m j)")
                 )
-            for t in range(PACK):
-                nc.tensor.matmul_mx(
-                    out=banks[t // 2][:, t % 2, :],
-                    lhsT=codes[:, t, :].bitcast(FP8X4),
-                    lhsT_scale=planes[:, t, :],
-                    rhs=words[:].bitcast(FP8X4),
-                    rhs_scale=scales[:],
-                    start=True,
-                    stop=True,
-                )
+                bank = psum.tile([P, 2, S], F32, name=name + "_bank%d" % b)
+                for u in range(2):
+                    nc.tensor.matmul_mx(
+                        out=bank[:, u, :],
+                        lhsT=codes[:, u * P : (u + 1) * P].bitcast(FP8X4),
+                        lhsT_scale=plane[:, u * P : (u + 1) * P],
+                        rhs=words[:].bitcast(FP8X4),
+                        rhs_scale=scales[:],
+                        start=True,
+                        stop=True,
+                    )
+                banks.append(bank)
             return banks
 
         xq_scales = gather_bytes("xq_scales", x_bytes, offs_sb, S)
-        xq_words = gather_words("xq_words", x_table, offs_sb, S)
         x2_scales = gather_bytes("x2_scales", x_bytes, two_sb, S)
+        xq_words = gather_words("xq_words", x_table, offs_sb, S)
         x2_words = gather_words("x2_words", x_table, two_sb, S)
 
-        y_banks = project("y", round_weight("w1_bf", w1_raw, 44), xq_words, xq_scales)
+        w1_bf = [sb("w1_bf%d" % b, [P, 2, P, PACK], BF16) for b in range(2)]
+        round_part(False, w1_bf[0], w1_raw[0], 0, 2)
+        round_part(False, w1_bf[1], w1_raw[0], 2, 4)
+        round_part(True, w1_bf[0], w1_raw[1], 0, 2)
+        round_part(False, w1_bf[1], w1_raw[1], 2, 4)
+        y_banks = project("y", [w1_bf[0][:], w1_bf[1][:]], xq_words, xq_scales)
+        w2_bf = sb("w2_bf", [P, PACK, P, PACK], BF16)
+        round_part(False, w2_bf, w2_raw[0], 0, 4)
         for t in range(PACK):
-            nc.scalar.activation(y_win[t][:, :S], y_banks[t // 2][:, t % 2, :], ACT.Copy)
+            nc.scalar.activation(y_win[t][:, :S], y_banks[t // 2][:, t % 2, :], ACT.Copy, scale=gs_sb[:, t : t + 1])
 
-        y_n1 = sb("y_n1", [P, PACK, S], F32)
-        y_n2 = sb("y_n2", [P, PACK, S], F32)
+        y_picked = sb("y_picked", [P, PACK, 2, S], F32)
+        diff = sb("diff", [P, PACK, 2, S], F32)
         for t in range(PACK):
-            nc.scalar.activation(y_n2[:, t, :], y_win[t][:].indirect(n2_sb[:]), ACT.Copy)
-            nc.scalar.activation(y_n1[:, t, :], y_win[t][:].indirect(n1_sb[:]), ACT.Copy)
+            nc.scalar.activation(y_picked[:, t, 0, :], y_win[t][:].indirect(n1_sb[:]), ACT.Copy)
+            nc.scalar.activation(y_picked[:, t, 1, :], y_win[t][:].indirect(n2_sb[:]), ACT.Copy)
+            own = y_win[t][:, :S].unsqueeze(1).to_broadcast([P, 2, S])
+            nc.gpsimd.tensor_tensor(diff[:, t], y_picked[:, t], own, ALU.subtract)
 
-        d_banks = project("d", round_weight("w2_bf", w2_raw, 64), x2_words, x2_scales)
-        for t in range(PACK):
-            nc.scalar.activation(d_win[t][:, :S], d_banks[t // 2][:, t % 2, :], ACT.Copy, scale=gs_sb[:, t : t + 1])
-
-        dk_picked = gather_bytes("dk_picked", d_bytes, k1_sb, H)
+        for part in w2_raw[1:]:
+            round_part(True, w2_bf, part, 0, 4)
+        d_banks = project("d", [w2_bf[:, 0:2], w2_bf[:, 2:4]], x2_words, x2_scales)
+        dk_picked = gather_bytes("dk_picked", d_bytes, k1_sb, H, tag="w2_bf")
         for i in range(4):
             nc.sync.dma_start(dk_scales[i:P:32, :].bitcast(I32), dk_picked[8 * i : P : 32, :].bitcast(I32))
-
-        diff1 = sb("diff1", [P, PACK, S], F32)
-        diff2 = sb("diff2", [P, PACK, S], F32)
-        for b in range(2):
-            pair = slice(2 * b, 2 * b + 2)
-            nc.vector.tensor_tensor(diff2[:, pair, :], y_n2[:, pair, :], y_banks[b][:], ALU.subtract)
-            nc.vector.tensor_tensor(diff1[:, pair, :], y_n1[:, pair, :], y_banks[b][:], ALU.subtract)
-
+        for t in range(PACK):
+            nc.vector.tensor_copy(d_win[t][:, :S], d_banks[t // 2][:, t % 2, :])
         dk_words = gather_words("dk_words", d_table, k1_sb, H)
 
         term1 = sb("term1", [P, PACK, S], F32)
-        for t in range(PACK):
-            nc.vector.tensor_tensor(term1[:, t, :], diff1[:, t, :], d_win[t][:, :S], ALU.mult)
+        nc.vector.tensor_tensor(term1[:, 0:2, :], d_banks[0][:], diff[:, 0:2, 0, :], ALU.mult)
+        for t in (2, 3):
+            nc.vector.tensor_tensor(term1[:, t, :], d_banks[1][:, t % 2, :], diff[:, t, 0, :], ALU.mult)
 
+        e_n4 = sb("e_n4", [P, PACK, S], F32)
         e_inv = sb("e_inv", [P, PACK, S], F32)
         for h in range(2):
             cols = slice(h * HALF, (h + 1) * HALF)
@@ -168,11 +170,10 @@ def tile_picked_twqflowbshare_none_p_kernel(
                 nc.scalar.activation(
                     d_n3[:, t, :], d_win[t][:].indirect(n3_sb[:, h * HALF // 16 : (h + 1) * HALF // 16]), ACT.Copy
                 )
-            term2 = sb("term2_%d" % h, [P, PACK, HALF], F32)
-            for b in range(2):
-                pair = slice(2 * b, 2 * b + 2)
+            term2 = sb("term2_%d" % h, [P, PACK, HALF], F32, tag="term2")
+            for tiles in ((slice(0, 4),), (slice(0, 2), slice(2, 4)))[h]:
                 nc.vector.scalar_tensor_tensor(
-                    term2[:, pair, :], d_n3[:, pair, :], 0.5, diff2[:, pair, cols], ALU.mult, ALU.mult
+                    term2[:, tiles, :], d_n3[:, tiles, :], 0.5, diff[:, tiles, 1, cols], ALU.mult, ALU.mult
                 )
             z_bf = sb("z_bf%d" % h, [P, HALF, PACK], BF16)
             nc.vector.tensor_tensor(
@@ -186,11 +187,12 @@ def tile_picked_twqflowbshare_none_p_kernel(
             nc.vector.quantize_mx(
                 out=z_codes[:].bitcast(FP8X4), scales=z_plane[:], in_=z_bf[:].rearrange("p j t -> p (j t)")
             )
-            banks = [psum.tile([P, 2, HALF], F32, name="h_bank%d_%d" % (h, b)) for b in range(2)]
+            tags = (("h_bank0", "h_bank1", "d_bank0", "d_bank1"), ("h_bank2", "h_bank3", "y_bank0", "y_bank1"))[h]
+            banks = [psum.tile([P, HALF], F32, name="h%d_%d" % (h, m), tag=tags[m]) for m in range(PACK)]
             for m in range(PACK):
                 rows = slice(m * P, (m + 1) * P)
                 nc.tensor.matmul_mx(
-                    out=banks[m // 2][:, m % 2, :],
+                    out=banks[m][:],
                     lhsT=dk_words[:, rows].bitcast(FP8X4),
                     lhsT_scale=dk_scales[:, rows],
                     rhs=z_codes[:].bitcast(FP8X4),
@@ -199,13 +201,11 @@ def tile_picked_twqflowbshare_none_p_kernel(
                     stop=True,
                 )
             for m in range(PACK):
-                nc.scalar.activation(e_win[m][:, cols], banks[m // 2][:, m % 2, :], ACT.Exp, scale=0.5 * 0.0625)
-            for b in range(2):
-                nc.scalar.activation(e_inv[:, 2 * b : 2 * b + 2, cols], banks[b][:], ACT.Exp, scale=-0.5 * 0.0625)
+                nc.scalar.activation(e_win[m][:, cols], banks[m][:], ACT.Exp, scale=0.5 * 0.0625)
+                if h == 1:
+                    nc.scalar.activation(e_n4[:, m, :], e_win[m][:].indirect(n4_sb[:]), ACT.Copy)
+                nc.scalar.activation(e_inv[:, m, cols], banks[m][:], ACT.Exp, scale=-0.5 * 0.0625)
 
-        e_n4 = sb("e_n4", [P, PACK, S], F32)
-        for m in range(PACK):
-            nc.scalar.activation(e_n4[:, m, :], e_win[m][:].indirect(n4_sb[:]), ACT.Copy)
         e_n45 = sb("e_n45", [P, PACK, S], F32)
         ratio = sb("ratio", [P, PACK, S], F32)
         for m in range(PACK + 1):

@@ -58,7 +58,6 @@ def tile_picked_twqflowbshare_none_p_kernel(
         nc.gpsimd.memset(dk_scales[:].bitcast(I32), 0)
         for win in d_win:
             nc.gpsimd.memset(win[:, S:], 0.0)
-        nc.gpsimd.dma_start(gs_sb[:], gs.rearrange("(p t) o -> p (t o)", t=PACK))
         nc.gpsimd.dma_start(d_bytes[0:P:8, :].bitcast(I32), d_scales[0].bitcast(I32))
 
         offs_sb = load_list("offs_sb", offs)
@@ -70,6 +69,7 @@ def tile_picked_twqflowbshare_none_p_kernel(
                 x_bytes[32 * q : 32 * q + 4, :].bitcast(I32), x_scales[0, 4 * q : 4 * q + 4, :].bitcast(I32)
             )
         w1_raw = [load_weight_part("w1_raw%d" % m0, w1, m0, m0 + 64) for m0 in (0, 64)]
+        nc.sync.dma_start(gs_sb[:], gs.rearrange("(p t) o -> p (t o)", t=PACK))
         w2_raw = [load_weight_part("w2_raw0", w2, 0, 32), load_weight_part("w2_raw32", w2, 32, 80)]
         k1_sb = load_list("k1_sb", k1)
         n1_sb = load_list("n1_sb", n1)
@@ -156,21 +156,23 @@ def tile_picked_twqflowbshare_none_p_kernel(
             nc.vector.tensor_copy(d_win[t][:, :S], d_banks[t // 2][:, t % 2, :])
         dk_words = gather_words("dk_words", d_table, k1_sb, H)
 
-        term1 = sb("term1", [P, PACK, S], F32)
+        term1 = sb("term1", [P, PACK, S], F32, tag="d_table")
         nc.vector.tensor_tensor(term1[:, 0:2, :], d_banks[0][:], diff[:, 0:2, 0, :], ALU.mult)
         for t in (2, 3):
             nc.vector.tensor_tensor(term1[:, t, :], d_banks[1][:, t % 2, :], diff[:, t, 0, :], ALU.mult)
+
+        d_picked = [sb("d_picked%d" % h, [P, PACK, HALF], F32) for h in range(2)]
+        for h in range(2):
+            entries = slice(h * HALF // 16, (h + 1) * HALF // 16)
+            for t in range(PACK):
+                nc.scalar.activation(d_picked[h][:, t, :], d_win[t][:].indirect(n3_sb[:, entries]), ACT.Copy)
 
         e_n4 = sb("e_n4", [P, PACK, S], F32)
         e_inv = sb("e_inv", [P, PACK, S], F32)
         for h in range(2):
             cols = slice(h * HALF, (h + 1) * HALF)
-            d_n3 = sb("d_n3_%d" % h, [P, PACK, HALF], F32)
-            for t in range(PACK):
-                nc.scalar.activation(
-                    d_n3[:, t, :], d_win[t][:].indirect(n3_sb[:, h * HALF // 16 : (h + 1) * HALF // 16]), ACT.Copy
-                )
-            term2 = sb("term2_%d" % h, [P, PACK, HALF], F32, tag="term2")
+            d_n3 = d_picked[h]
+            term2 = sb("term2_%d" % h, [P, PACK, HALF], F32, tag=("y_picked", "d_picked0")[h])
             for tiles in ((slice(0, 4),), (slice(0, 2), slice(2, 4)))[h]:
                 nc.vector.scalar_tensor_tensor(
                     term2[:, tiles, :], d_n3[:, tiles, :], 0.5, diff[:, tiles, 1, cols], ALU.mult, ALU.mult

from contextlib import ExitStack

import concourse.mybir as mybir

K, T, S, H, G = 512, 1024, 256, 512, 2048
FLOPS = 3 * 2 * K * H * S

F32 = mybir.dt.float32
BF16 = mybir.dt.bfloat16
I32 = mybir.dt.int32
U32 = mybir.dt.uint32
U16 = mybir.dt.uint16
U8 = mybir.dt.uint8
FP8X4 = mybir.dt.float8_e4m3fn_x4
ACT = mybir.ActivationFunctionType
ALU = mybir.AluOpType

P = 128
PACK = 4
WINDOW = 2 * S
HALF = S // 2


def tile_picked_twqflowbshare_none_p_kernel(
    tc, x_words, x_scales, w1, w2, gs, d_words, d_scales, offs, two, n1, n2, n3, k1, n4, n5, out
):
    nc = tc.nc
    with ExitStack() as ctx:
        keep = ctx.enter_context(tc.tile_pool(name="keep", bufs=1))
        psum = ctx.enter_context(tc.psum_pool(name="psum", bufs=1))

        def sb(name, shape, dtype, tag=None):
            return keep.tile(shape, dtype, name=name, tag=tag or name, align_bytes=64)

        def load_list(name, src):
            tile = keep.tile([P, src.shape[1]], U16, name=name)
            nc.sync.dma_start(tile[:], src)
            return tile

        def load_weight_part(name, w, m0, m1):
            raw = sb(name, [P, PACK, PACK * (m1 - m0)], F32)
            nc.sync.dma_start(raw[:], w.rearrange("(p j) c -> p j c", j=PACK)[:, :, PACK * m0 : PACK * m1])
            return raw, m0, m1

        x_bytes = sb("x_bytes", [P, T], U8)
        d_bytes = sb("d_bytes", [P, G], U8)
        dk_scales = sb("dk_scales", [P, H], U8)
        y_win = [sb("y_win%d" % t, [P, WINDOW], F32) for t in range(PACK)]
        d_win = [sb("d_win%d" % t, [P, WINDOW], F32) for t in range(PACK)]
        e_win = [sb("e_win%d" % m, [P, S + 16], F32) for m in range(PACK)]
        half = sb("half", [P, 1], F32)
        gs_sb = sb("gs_sb", [P, PACK], F32)
        nc.gpsimd.memset(x_bytes[:].bitcast(I32), 0)
        nc.vector.memset(d_bytes[:].bitcast(I32), 0)
        for win in y_win + e_win:
            nc.vector.memset(win[:, S:], 0.0)
        nc.vector.memset(half[:], 0.5)
        nc.gpsimd.memset(dk_scales[:].bitcast(I32), 0)
        for win in d_win:
            nc.gpsimd.memset(win[:, S:], 0.0)
        nc.gpsimd.dma_start(d_bytes[0:P:8, :].bitcast(I32), d_scales[0].bitcast(I32))

        offs_sb = load_list("offs_sb", offs)
        two_sb = load_list("two_sb", two)
        x_table = sb("x_table", [P, T], I32)
        nc.sync.dma_start(x_table[:], x_words[0].rearrange("p n t -> p (n t)").bitcast(I32))
        for q in range(4):
            nc.sync.dma_start(
                x_bytes[32 * q : 32 * q + 4, :].bitcast(I32), x_scales[0, 4 * q : 4 * q + 4, :].bitcast(I32)
            )
        w1_raw = [load_weight_part("w1_raw%d" % m0, w1, m0, m0 + 64) for m0 in (0, 64)]
        nc.sync.dma_start(gs_sb[:], gs.rearrange("(p t) o -> p (t o)", t=PACK))
        w2_raw = [load_weight_part("w2_raw0", w2, 0, 32), load_weight_part("w2_raw32", w2, 32, 80)]
        k1_sb = load_list("k1_sb", k1)
        n1_sb = load_list("n1_sb", n1)
        n2_sb = load_list("n2_sb", n2)
        w2_raw.append(load_weight_part("w2_raw80", w2, 80, 128))
        d_table = sb("d_table", [P, G], I32)
        nc.sync.dma_start(d_table[:], d_words[0].rearrange("p n t -> p (n t)").bitcast(I32))
        n3_sb = load_list("n3_sb", n3)
        n4_sb = load_list("n4_sb", n4)
        n5_sb = load_list("n5_sb", n5)

        def gather_bytes(name, table, offsets, n, tag=None):
            picked = sb(name, [P, n], U8, tag=tag)
            nc.vector.tensor_copy(picked[:], table[:].indirect(offsets[:]))
            return picked

        def gather_words(name, table, offsets, n, tag=None):
            picked = sb(name, [P, n], U32, tag=tag)
            nc.vector.tensor_copy(picked[:], table[:].bitcast(U32).indirect(offsets[:]))
            return picked

        def round_part(on_vector, grouped, part, t0, t1):
            raw, m0, m1 = part
            src = raw[:].rearrange("p j (m t) -> p m j t", t=PACK)[:, :, :, t0:t1]
            dst = grouped[:, :, m0:m1, :].rearrange("p t m j -> p m j t")
            if on_vector:
                nc.vector.tensor_copy(dst, src)
            else:
                nc.scalar.activation(dst, src, ACT.Copy)

        def project(name, pairs, words, scales):
            banks = []
            for b in range(2):
                codes = sb(name + "_codes%d" % b, [P, 2 * P], U32)
                plane = sb(name + "_plane%d" % b, [P, 2 * P], U8)
                nc.vector.quantize_mx(
                    out=codes[:].bitcast(FP8X4), scales=plane[:], in_=pairs[b].rearrange("p t m j -> p (t m j)")
                )
                bank = psum.tile([P, 2, S], F32, name=name + "_bank%d" % b)
                for u in range(2):
                    nc.tensor.matmul_mx(
                        out=bank[:, u, :],
                        lhsT=codes[:, u * P : (u + 1) * P].bitcast(FP8X4),
                        lhsT_scale=plane[:, u * P : (u + 1) * P],
                        rhs=words[:].bitcast(FP8X4),
                        rhs_scale=scales[:],
                        start=True,
                        stop=True,
                    )
                banks.append(bank)
            return banks

        xq_scales = gather_bytes("xq_scales", x_bytes, offs_sb, S)
        x2_scales = gather_bytes("x2_scales", x_bytes, two_sb, S)
        xq_words = gather_words("xq_words", x_table, offs_sb, S)
        x2_words = gather_words("x2_words", x_table, two_sb, S)

        w1_bf = [sb("w1_bf%d" % b, [P, 2, P, PACK], BF16) for b in range(2)]
        round_part(False, w1_bf[0], w1_raw[0], 0, 2)
        round_part(False, w1_bf[1], w1_raw[0], 2, 4)
        round_part(True, w1_bf[0], w1_raw[1], 0, 2)
        round_part(False, w1_bf[1], w1_raw[1], 2, 4)
        y_banks = project("y", [w1_bf[0][:], w1_bf[1][:]], xq_words, xq_scales)
        w2_bf = sb("w2_bf", [P, PACK, P, PACK], BF16)
        round_part(False, w2_bf, w2_raw[0], 0, 4)
        for t in range(PACK):
            nc.scalar.activation(y_win[t][:, :S], y_banks[t // 2][:, t % 2, :], ACT.Copy, scale=gs_sb[:, t : t + 1])

        y_picked = sb("y_picked", [P, PACK, 2, S], F32)
        diff = sb("diff", [P, PACK, 2, S], F32)
        for t in range(PACK):
            nc.scalar.activation(y_picked[:, t, 0, :], y_win[t][:].indirect(n1_sb[:]), ACT.Copy)
            nc.scalar.activation(y_picked[:, t, 1, :], y_win[t][:].indirect(n2_sb[:]), ACT.Copy)
            own = y_win[t][:, :S].unsqueeze(1).to_broadcast([P, 2, S])
            nc.gpsimd.tensor_tensor(diff[:, t], y_picked[:, t], own, ALU.subtract)

        for part in w2_raw[1:]:
            round_part(True, w2_bf, part, 0, 4)
        d_banks = project("d", [w2_bf[:, 0:2], w2_bf[:, 2:4]], x2_words, x2_scales)
        dk_picked = gather_bytes("dk_picked", d_bytes, k1_sb, H, tag="w2_bf")
        for i in range(4):
            nc.sync.dma_start(dk_scales[i:P:32, :].bitcast(I32), dk_picked[8 * i : P : 32, :].bitcast(I32))
        for t in range(PACK):
            nc.vector.tensor_copy(d_win[t][:, :S], d_banks[t // 2][:, t % 2, :])
        dk_words = gather_words("dk_words", d_table, k1_sb, H)

        term1 = sb("term1", [P, PACK, S], F32, tag="d_table")
        nc.vector.tensor_tensor(term1[:, 0:2, :], d_banks[0][:], diff[:, 0:2, 0, :], ALU.mult)
        for t in (2, 3):
            nc.vector.tensor_tensor(term1[:, t, :], d_banks[1][:, t % 2, :], diff[:, t, 0, :], ALU.mult)

        d_picked = [sb("d_picked%d" % h, [P, PACK, HALF], F32) for h in range(2)]
        for h in range(2):
            entries = slice(h * HALF // 16, (h + 1) * HALF // 16)
            for t in range(PACK):
                nc.scalar.activation(d_picked[h][:, t, :], d_win[t][:].indirect(n3_sb[:, entries]), ACT.Copy)

        e_n4 = sb("e_n4", [P, PACK, S], F32)
        e_inv = sb("e_inv", [P, PACK, S], F32)
        for h in range(2):
            cols = slice(h * HALF, (h + 1) * HALF)
            d_n3 = d_picked[h]
            term2 = sb("term2_%d" % h, [P, PACK, HALF], F32, tag=("y_picked", "d_picked0")[h])
            for tiles in ((slice(0, 4),), (slice(0, 2), slice(2, 4)))[h]:
                nc.vector.scalar_tensor_tensor(
                    term2[:, tiles, :], d_n3[:, tiles, :], 0.5, diff[:, tiles, 1, cols], ALU.mult, ALU.mult
                )
            z_bf = sb("z_bf%d" % h, [P, HALF, PACK], BF16)
            nc.vector.tensor_tensor(
                z_bf[:].rearrange("p (c i) t -> p c t i", i=4),
                term1[:, :, cols].rearrange("p t (c i) -> p c t i", i=4),
                term2[:].rearrange("p t (c i) -> p c t i", i=4),
                ALU.add,
            )
            z_codes = sb("z_codes%d" % h, [P, HALF], U32)
            z_plane = sb("z_plane%d" % h, [P, HALF], U8)
            nc.vector.quantize_mx(
                out=z_codes[:].bitcast(FP8X4), scales=z_plane[:], in_=z_bf[:].rearrange("p j t -> p (j t)")
            )
            tags = (("h_bank0", "h_bank1", "d_bank0", "d_bank1"), ("h_bank2", "h_bank3", "y_bank0", "y_bank1"))[h]
            banks = [psum.tile([P, HALF], F32, name="h%d_%d" % (h, m), tag=tags[m]) for m in range(PACK)]
            for m in range(PACK):
                rows = slice(m * P, (m + 1) * P)
                nc.tensor.matmul_mx(
                    out=banks[m][:],
                    lhsT=dk_words[:, rows].bitcast(FP8X4),
                    lhsT_scale=dk_scales[:, rows],
                    rhs=z_codes[:].bitcast(FP8X4),
                    rhs_scale=z_plane[:],
                    start=True,
                    stop=True,
                )
            for m in range(PACK):
                nc.scalar.activation(e_win[m][:, cols], banks[m][:], ACT.Exp, scale=0.5 * 0.0625)
                if h == 1:
                    nc.scalar.activation(e_n4[:, m, :], e_win[m][:].indirect(n4_sb[:]), ACT.Copy)
                nc.scalar.activation(e_inv[:, m, cols], banks[m][:], ACT.Exp, scale=-0.5 * 0.0625)

        e_n45 = sb("e_n45", [P, PACK, S], F32)
        ratio = sb("ratio", [P, PACK, S], F32)
        for m in range(PACK + 1):
            if m < PACK:
                nc.vector.tensor_tensor(e_n45[:, m, :], e_win[m][:].indirect(n5_sb[:]), e_n4[:, m, :], ALU.add)
            if m > 0:
                nc.vector.tensor_tensor(ratio[:, m - 1, :], e_n45[:, m - 1, :], e_inv[:, m - 1, :], ALU.mult)
        root = sb("root", [P, PACK, S], F32)
        res = sb("res", [P, PACK, S], F32)
        for m in range(PACK):
            nc.scalar.activation(root[:, m, :], ratio[:, m, :], ACT.Abs_reciprocal_sqrt, scale=0.5, bias=half[:])
            nc.vector.tensor_tensor(res[:, m, :], root[:, m, :], root[:, m, :], ALU.mult)
            nc.sync.dma_start(out[m * P : (m + 1) * P, :], res[:, m, :])
